import numpy as np
import ml_dtypes


def mxq(x, axis, fmt="e4m3"):
    dtype, down = {"e4m3": (ml_dtypes.float8_e4m3fn, 7), "e5m2": (ml_dtypes.float8_e5m2, 14)}[fmt]
    v = np.moveaxis(np.asarray(x, np.float32).astype(ml_dtypes.bfloat16).astype(np.float64), axis, -1)
    blocks = v.reshape(v.shape[:-1] + (-1, 32))
    amax = np.abs(blocks).max(-1, keepdims=True)
    byte = np.maximum(np.where(amax > 0, np.frexp(amax)[1] - 1 + 127, 0) - down, 1)
    scale = np.exp2(byte - 127.0)
    codes = (blocks / scale).astype(np.float32).astype(dtype).astype(np.float64)
    return np.moveaxis((codes * scale).reshape(v.shape), -1, axis)


WIDE = False


def mx_kscale(k):
    if not WIDE:
        return np.ones(k)
    levels = np.array([10, -10, 5, -5, 0])
    if k % 512:
        return np.exp2(np.random.permutation(np.resize(levels, k // 32))).repeat(32)
    a = np.empty((k // 512, 16))
    for p in range(k // 512):
        a[p, :8] = np.random.permutation(np.resize(levels, 8))
        for g in range(8):
            far = levels[np.abs(levels - a[p, g]) >= 10]
            a[p, g + 8] = far[np.random.randint(len(far))]
    return np.exp2(a.ravel()).repeat(32)


def f64(x):
    return np.asarray(x).astype(np.float64)


def striped(idx):
    return np.tile(np.asarray(idx).reshape(-1, 16).T, (8, 1)).astype(np.uint16)


def unstriped(offs):
    return offs[:16].T.reshape(-1).astype(np.int64)


E2M1 = np.array([0.0, 0.5, 1.0, 1.5, 2.0, 3.0, 4.0, 6.0, -0.0, -0.5, -1.0, -1.5, -2.0, -3.0, -4.0, -6.0])


def pack_weight(w, fmt):
    k, n = w.shape
    w = f64(np.asarray(w, np.float32).astype(ml_dtypes.bfloat16)).reshape(k // 32, 32, n)
    amax = np.abs(w).max(1)
    if fmt == "e4m3":
        byte = np.frexp(amax)[1] - 1 + 127 - 7
    else:
        mant, ex = np.frexp(amax / 6.0)
        byte = np.where(mant > 0.5, ex, ex - 1) + 127
    byte = np.clip(np.where(amax > 0, byte, 1), 1, 254)
    scaled = (w * np.exp2(127.0 - byte)[:, None, :]).reshape(k, n).astype(np.float32)
    by_word = np.ascontiguousarray(scaled.reshape(k // 512, 128, 4, n).transpose(0, 1, 3, 2))
    if fmt == "e4m3":
        words = by_word.astype(ml_dtypes.float8_e4m3fn).view(np.uint8)
    else:
        c = by_word.astype(ml_dtypes.float4_e2m1fn).view(np.uint8) & 0xF
        words = (c[..., 0::2] | (c[..., 1::2] << 4)).reshape(k // 512, 128, 2 * n)
    return np.ascontiguousarray(words), np.ascontiguousarray(byte.astype(np.uint8).reshape(k // 512, 16, n))


def unpack_weight(words, scales, fmt):
    g, _, n = scales.shape
    words = np.ascontiguousarray(words).reshape(g, 128, n, -1)
    if fmt == "e4m3":
        vals = words.view(ml_dtypes.float8_e4m3fn).astype(np.float64)
    else:
        nib = np.empty((g, 128, n, 4), np.uint8)
        nib[..., 0::2] = words & 0xF
        nib[..., 1::2] = words >> 4
        vals = E2M1[nib]
    vals = vals * np.repeat(np.exp2(scales.astype(np.float64) - 127.0), 8, axis=1)[..., None]
    return vals.transpose(0, 1, 3, 2).reshape(g * 512, n)


def sigmoid(v):
    return 1.0 / (1.0 + np.exp(-v))


D, E, T, I, Q, G = 512, 512, 2048, 512, 128, 32


def setup_inputs():
    n = np.random.standard_normal
    idx = np.random.permutation(T)[:I]
    fd = mx_kscale(D)
    fe = mx_kscale(E)
    fi = mx_kscale(I)
    ti = np.ones(T)
    ti[idx] = fi
    keysp = pack_weight(n((D, T)) / fd[:, None], "e2m1")
    valsp = pack_weight(n((E, T)) / fe[:, None], "e2m1")
    return {
        "query": (n((D, Q)) * 0.7 / np.sqrt(D) * fd[:, None]).astype(np.float32),
        "keys_words": keysp[0],
        "keys_scales": keysp[1],
        "th": (np.random.uniform(-0.2, 0.2, (Q, 1))).astype(np.float32),
        "steep": (np.random.uniform(2.0, 8.0, (Q, 1))).astype(np.float32),
        "gout": (n((E, Q)) * 1 / np.sqrt(E) * fe[:, None]).astype(np.float32),
        "vals_words": valsp[0],
        "vals_scales": valsp[1],
        "size": (np.random.uniform(0.5, 2.0, (1, I))).astype(np.float32),
        "fs": (np.random.uniform(128.0, 512.0, (1, I)) * fi).astype(np.float32),
        "keyrows": (n((D, T)) / ti).astype(np.float32),
        "res": (n((Q, D)) * 4.0).astype(np.float32),
        "offs": striped(idx),
    }


def reference(query, keys_words, keys_scales, th, steep, gout, vals_words, vals_scales, size, fs, keyrows, res, offs):
    idx = unstriped(offs)
    keysu = unpack_weight(keys_words, keys_scales, "e2m1")
    valsu = unpack_weight(vals_words, vals_scales, "e2m1")
    queryq = mxq(f64(query), 0, "e4m3")
    keysidxg = keysu[:, idx]
    a = queryq.T @ keysidxg
    s = a.reshape(Q, G, I // G).mean(axis=2)
    gt = sigmoid((s - f64(th)) * f64(steep))
    gr = np.repeat(gt, I // G, axis=1)
    r = np.exp(a - np.max(a, axis=1, keepdims=True))
    p = r * gr
    z = np.sum(p, axis=1, keepdims=True)
    goutq = mxq(f64(gout), 0, "e4m3")
    valsidxg = valsu[:, idx]
    c0 = goutq.T @ valsidxg
    dz = np.sum(c0 * p * f64(size) / np.square(z) * (-1.0), axis=1, keepdims=True)
    dp = c0 / z * f64(size) + dz
    dr = dp * gr
    dgr = dp * r
    dgt = dgr.reshape(Q, G, I // G).sum(axis=2)
    ds = dgt * gt * (1.0 - gt) * f64(steep)
    e1 = ds / 16.0
    r1 = np.repeat(e1, I // G, axis=1)
    da = dr * r + r1
    gs = da * f64(fs)
    gt1 = gs.T
    kt = f64(keyrows)[:, idx].T
    gt1q = mxq(gt1, 0, "e4m3")
    ktq = mxq(kt, 0, "e4m3")
    gq = gt1q.T @ ktq
    y = gq + f64(res)
    return y

@@ -1,0 +1,201 @@
+from contextlib import ExitStack
+
+import concourse.mybir as mybir
+from concourse.masks import make_identity
+
+D, E, T, I, Q, G = 512, 512, 2048, 512, 128, 32
+FLOPS = 2 * Q * I * (D + E + D)
+
+F32 = mybir.dt.float32
+BF16 = mybir.dt.bfloat16
+I32 = mybir.dt.int32
+U32 = mybir.dt.uint32
+U16 = mybir.dt.uint16
+U8 = mybir.dt.uint8
+FP8X4 = mybir.dt.float8_e4m3fn_x4
+FP4X4 = mybir.dt.float4_e2m1fn_x4
+ALU = mybir.AluOpType
+ACT = mybir.ActivationFunctionType
+AXIS = mybir.AxisListType
+
+P = 128
+PACK = 4
+PAGE = I // G
+BLOCKS = D // P
+
+
+def tile_attend_bpagegate_q_kernel(tc, query, keys_words, keys_scales, th, steep, gout, vals_words, vals_scales,
+                                    size, fs, keyrows, res, offs, out):
+    nc = tc.nc
+    with ExitStack() as ctx:
+        sb = ctx.enter_context(tc.tile_pool(name="sb", bufs=1))
+        ps = ctx.enter_context(tc.psum_pool(name="ps", bufs=1))
+
+        def load_scales(name, scales, engine):
+            plane = sb.tile([P, T], U8, name=name, align_bytes=64)
+            engine.memset(plane[:].bitcast(I32), 0)
+            for quad in range(4):
+                nc.sync.dma_start(plane[32 * quad : 32 * quad + 4, :].bitcast(I32),
+                                  scales[0, 4 * quad : 4 * quad + 4, :].bitcast(I32))
+            return plane
+
+        def load_words(name, words):
+            pool_words = sb.tile([P, T], U16, name=name, align_bytes=64)
+            nc.sync.dma_start(pool_words[:].bitcast(I32), words[0].bitcast(I32))
+            return pool_words
+
+        def load_rows(name, rows):
+            raw = sb.tile([P, PACK, Q], F32, name=name)
+            nc.sync.dma_start(raw[:], rows.rearrange("(p j) q -> p j q", j=PACK))
+            return raw
+
+        def load_block(b):
+            block = sb.tile([P, T], F32, name="rows%d" % b)
+            nc.sync.dma_start(block[:], keyrows[b * P : (b + 1) * P, :])
+            return block
+
+        offsets = sb.tile([P, I // 16], U16, name="offsets")
+        nc.sync.dma_start(offsets[:], offs)
+        key_plane = load_scales("key_plane", keys_scales, nc.gpsimd)
+        key_words = load_words("key_words", keys_words)
+        query_raw = load_rows("query_raw", query)
+        val_words = load_words("val_words", vals_words)
+        val_plane = load_scales("val_plane", vals_scales, nc.vector)
+        gout_raw = load_rows("gout_raw", gout)
+        rows = [load_block(0), load_block(1)]
+        steep_col = sb.tile([P, 1], F32, name="steep_col")
+        nc.gpsimd.dma_start(steep_col[:], steep)
+        th_col = sb.tile([P, 1], F32, name="th_col")
+        nc.gpsimd.dma_start(th_col[:], th)
+        size_rows = sb.tile([P, P], F32, name="size_rows")
+        nc.gpsimd.memset(size_rows[:], 0.0)
+        nc.sync.dma_start(size_rows[0 : I // P, :], size.rearrange("o (c p) -> (o c) p", p=P))
+        fs_cols = sb.tile([P, PACK], F32, name="fs_cols")
+        nc.sync.dma_start(fs_cols[:], fs.rearrange("o (p r) -> p (o r)", r=PACK))
+        for b in range(2, BLOCKS):
+            rows.append(load_block(b))
+        res_sb = sb.tile([P, D], F32, name="res_sb")
+        nc.sync.dma_start(res_sb[:], res)
+
+        ident = sb.tile([P, P], F32, name="ident")
+        make_identity(nc, ident[:])
+        size_ps = ps.tile([P, P], F32, name="size_ps", tag="gq_ps", bufs=2)
+        nc.tensor.transpose(size_ps[:], size_rows[:], ident[:])
+        size_cols = sb.tile([P, I // P], F32, name="size_cols")
+        nc.scalar.copy(size_cols[:], size_ps[:, 0 : I // P])
+
+        def quantise(name, grouped, width):
+            codes = sb.tile([P, width], U32, name=name + "_codes", align_bytes=64)
+            scales = sb.tile([P, width], U8, name=name + "_scales", align_bytes=64)
+            nc.vector.quantize_mx(out=codes[:].bitcast(FP8X4), scales=scales[:], in_=grouped)
+            return codes, scales
+
+        def interleave(name, raw):
+            grouped = sb.tile([P, Q, PACK], BF16, name=name, align_bytes=64)
+            nc.scalar.copy(grouped[:], raw[:].rearrange("p j q -> p q j"))
+            return grouped[:].rearrange("p q j -> p (q j)")
+
+        def gather(name, window, dtype):
+            picked = sb.tile([P, I], dtype, name=name, align_bytes=64)
+            nc.vector.tensor_copy(picked[:], window[:].indirect(offsets[:]))
+            return picked
+
+        query_grouped = interleave("query_grouped", query_raw)
+        key_scales = gather("key_scales", key_plane, U8)
+        key_codes = gather("key_codes", key_words, U16)
+        q_codes, q_scales = quantise("q", query_grouped, Q)
+        a_ps = ps.tile([P, I], F32, name="a_ps")
+        nc.tensor.matmul_mx(out=a_ps[:], lhsT=q_codes[:].bitcast(FP8X4), lhsT_scale=q_scales[:],
+                            rhs=key_codes[:].bitcast(FP4X4), rhs_scale=key_scales[:], start=True, stop=True)
+
+        gout_grouped = interleave("gout_grouped", gout_raw)
+        val_codes = gather("val_codes", val_words, U16)
+        val_scales = gather("val_scales", val_plane, U8)
+        g_codes, g_scales = quantise("g", gout_grouped, Q)
+        c0t_ps = ps.tile([P, I // P, Q], F32, name="c0t_ps")
+        for c in range(I // P):
+            cols = slice(c * P, (c + 1) * P)
+            nc.tensor.matmul_mx(out=c0t_ps[:, c, :], lhsT=val_codes[:, cols].bitcast(FP4X4), lhsT_scale=val_scales[:, cols],
+                                rhs=g_codes[:].bitcast(FP8X4), rhs_scale=g_scales[:], start=True, stop=True)
+
+        neg_slope = sb.tile([P, 1], F32, name="neg_slope")
+        nc.scalar.activation(neg_slope[:], steep_col[:], ACT.Copy, scale=-1.0 / PAGE)
+        slope = sb.tile([P, 1], F32, name="slope")
+        nc.scalar.activation(slope[:], steep_col[:], ACT.Copy, scale=1.0 / PAGE)
+        th_steep = sb.tile([P, 1], F32, name="th_steep")
+        nc.scalar.activation(th_steep[:], th_col[:], ACT.Copy, scale=steep_col[:])
+
+        page_sum = sb.tile([P, G], F32, name="page_sum")
+        nc.vector.tensor_reduce(page_sum[:], a_ps[:].rearrange("q (g j) -> q g j", j=PAGE), AXIS.X, ALU.add)
+        neg_max = sb.tile([P, 1], F32, name="neg_max")
+        nc.vector.tensor_reduce(neg_max[:], a_ps[:], AXIS.X, ALU.max, negate=True)
+        odds = sb.tile([P, G], F32, name="odds")
+        nc.scalar.activation(odds[:], page_sum[:], ACT.Exp, bias=th_steep[:], scale=neg_slope[:])
+        denom = sb.tile([P, G], F32, name="denom")
+        nc.scalar.activation(denom[:], odds[:], ACT.Identity, bias=1.0)
+        r = sb.tile([P, PACK, P], F32, name="r")
+        nc.scalar.activation(r[:], a_ps[:].rearrange("q (s r) -> q r s", r=PACK), ACT.Exp, bias=neg_max[:])
+        gate = sb.tile([P, G], F32, name="gate")
+        nc.vector.reciprocal(gate[:], denom[:])
+        gate4 = sb.tile([P, G, PACK], F32, name="gate4")
+        nc.scalar.copy(gate4[:], gate[:].unsqueeze(2).broadcast_to([P, G, PACK]))
+        gate_slope = sb.tile([P, G], F32, name="gate_slope")
+        nc.scalar.activation(gate_slope[:], gate[:], ACT.Identity, bias=slope[:], scale=neg_slope[:])
+
+        ut = sb.tile([P, I // P, Q], F32, name="ut")
+        for c in range(I // P):
+            nc.scalar.activation(ut[:, c, :], c0t_ps[:, c, :], ACT.Copy, scale=size_cols[:, c : c + 1])
+        u_ps = ps.tile([P, I], F32, name="u_ps")
+        for c in range(I // P):
+            nc.tensor.transpose(u_ps[:, c * P : (c + 1) * P], ut[:, c, :], ident[:])
+
+        p = sb.tile([P, PACK, P], F32, name="p")
+        z = sb.tile([P, 1], F32, name="z")
+        gate_slots = gate4[:].rearrange("q g j -> q (g j)").unsqueeze(1).broadcast_to([P, PACK, P])
+        nc.vector.scalar_tensor_tensor(p[:], r[:], 1.0, gate_slots, ALU.mult, ALU.mult, accum_out=z[:])
+        inv_z = sb.tile([P, 1], F32, name="inv_z")
+        nc.vector.reciprocal(inv_z[:], z[:])
+        pu = sb.tile([P, PACK, P], F32, name="pu")
+        pu_sum = sb.tile([P, 1], F32, name="pu_sum")
+        nc.vector.scalar_tensor_tensor(pu[:], u_ps[:].rearrange("q (s r) -> q r s", r=PACK), inv_z[:], p[:],
+                                       ALU.mult, ALU.mult, accum_out=pu_sum[:])
+        dz = sb.tile([P, 1], F32, name="dz")
+        nc.vector.tensor_scalar(dz[:], pu_sum[:], inv_z[:], -1.0, ALU.mult, ALU.mult)
+        w = sb.tile([P, PACK, P], F32, name="w")
+        nc.vector.scalar_tensor_tensor(w[:], p[:], dz[:], pu[:], ALU.mult, ALU.add)
+        w_page = sb.tile([P, G], F32, name="w_page")
+        nc.vector.tensor_reduce(w_page[:], w[:].rearrange("q r (g j) -> q g r j", j=PACK), AXIS.XY, ALU.add)
+        r1 = sb.tile([P, G, PACK], F32, name="r1")
+        nc.vector.tensor_tensor(r1[:], w_page[:].unsqueeze(2).broadcast_to([P, G, PACK]),
+                                gate_slope[:].unsqueeze(2).broadcast_to([P, G, PACK]), ALU.mult)
+        dat_ps = ps.tile([P, PACK, Q], F32, name="dat_ps")
+        for place in range(PACK):
+            nc.tensor.matmul(dat_ps[:, place, :], w[:, place, :], ident[:], start=(place == 0), stop=False, is_transpose=True)
+        for place in range(PACK):
+            nc.tensor.matmul(dat_ps[:, place, :], r1[:].rearrange("q g j -> q (g j)"), ident[:],
+                             start=False, stop=(place == PACK - 1), is_transpose=True)
+        gs_grouped = sb.tile([P, Q, PACK], BF16, name="gs_grouped", align_bytes=64)
+        nc.vector.tensor_tensor(gs_grouped[:], dat_ps[:].rearrange("s r q -> s q r"),
+                                fs_cols[:].unsqueeze(1).broadcast_to([P, Q, PACK]), ALU.mult)
+        gs_codes, gs_scales = quantise("gs", gs_grouped[:].rearrange("s q r -> s (q r)"), Q)
+
+        quantised_rows = []
+        for b in range(BLOCKS):
+            picked = gather("picked%d" % b, rows[b], BF16)
+            pairs = picked[:].bitcast(F32)
+            kt_ps = ps.tile([P, 2, P], F32, name="kt_ps", tag="kt_ps", bufs=2)
+            for half in range(2):
+                nc.tensor.transpose(kt_ps[:, half, :], pairs[:, half : I // 2 : 2], ident[:])
+            kt_grouped = sb.tile([P, P * PACK], BF16, name="kt_grouped%d" % b, align_bytes=64)
+            nc.scalar.copy(kt_grouped[:].bitcast(F32).rearrange("s (d h) -> s d h", h=2), kt_ps[:].rearrange("s h d -> s d h"))
+            quantised_rows.append(quantise("kt%d" % b, kt_grouped[:], P))
+
+        for b in range(BLOCKS):
+            cols = slice(b * P, (b + 1) * P)
+            kt_codes, kt_scales = quantised_rows[b]
+            gq_ps = ps.tile([P, P], F32, name="gq_ps", tag="gq_ps", bufs=2)
+            nc.tensor.matmul_mx(out=gq_ps[:], lhsT=gs_codes[:].bitcast(FP8X4), lhsT_scale=gs_scales[:],
+                                rhs=kt_codes[:].bitcast(FP8X4), rhs_scale=kt_scales[:], start=True, stop=True)
+            y = sb.tile([P, P], F32, name="y%d" % b)
+            nc.vector.tensor_tensor(y[:], gq_ps[:], res_sb[:, cols], ALU.add)
+            nc.sync.dma_start(out[:, cols], y[:])

@@ -32,7 +32,7 @@ def tile_attend_bpagegate_q_kernel(tc, query, keys_words, keys_scales, th, steep
         ps = ctx.enter_context(tc.psum_pool(name="ps", bufs=1))
 
         def load_scales(name, scales, engine):
-            plane = sb.tile([P, T], U8, name=name, align_bytes=64)
+            plane = sb.tile([P, T], U8, name=name, tag=name, align_bytes=64)
             engine.memset(plane[:].bitcast(I32), 0)
             for quad in range(4):
                 nc.sync.dma_start(plane[32 * quad : 32 * quad + 4, :].bitcast(I32),
@@ -45,12 +45,12 @@ def tile_attend_bpagegate_q_kernel(tc, query, keys_words, keys_scales, th, steep
             return pool_words
 
         def load_rows(name, rows):
-            raw = sb.tile([P, PACK, Q], F32, name=name)
+            raw = sb.tile([P, PACK, Q], F32, name=name, tag=name)
             nc.sync.dma_start(raw[:], rows.rearrange("(p j) q -> p j q", j=PACK))
             return raw
 
         def load_block(b):
-            block = sb.tile([P, T], F32, name="rows%d" % b)
+            block = sb.tile([P, T], F32, name="rows%d" % b, tag="rows%d" % b, align_bytes=64)
             nc.sync.dma_start(block[:], keyrows[b * P : (b + 1) * P, :])
             return block
 
@@ -60,110 +60,127 @@ def tile_attend_bpagegate_q_kernel(tc, query, keys_words, keys_scales, th, steep
         key_words = load_words("key_words", keys_words)
         query_raw = load_rows("query_raw", query)
         val_words = load_words("val_words", vals_words)
+        size_rows = sb.tile([P, P], F32, name="size_rows")
+        nc.vector.memset(size_rows[:], 0.0)
+        nc.sync.dma_start(size_rows[0 : I // P, :], size.rearrange("o (c p) -> (o c) p", p=P))
         val_plane = load_scales("val_plane", vals_scales, nc.vector)
         gout_raw = load_rows("gout_raw", gout)
-        rows = [load_block(0), load_block(1)]
+        rows = [load_block(0)]
         steep_col = sb.tile([P, 1], F32, name="steep_col")
         nc.gpsimd.dma_start(steep_col[:], steep)
-        th_col = sb.tile([P, 1], F32, name="th_col")
+        th_col = sb.tile([P, 1], F32, name="th_col", tag="th_col")
         nc.gpsimd.dma_start(th_col[:], th)
-        size_rows = sb.tile([P, P], F32, name="size_rows")
-        nc.gpsimd.memset(size_rows[:], 0.0)
-        nc.sync.dma_start(size_rows[0 : I // P, :], size.rearrange("o (c p) -> (o c) p", p=P))
+        for b in range(1, BLOCKS):
+            rows.append(load_block(b))
         fs_cols = sb.tile([P, PACK], F32, name="fs_cols")
         nc.sync.dma_start(fs_cols[:], fs.rearrange("o (p r) -> p (o r)", r=PACK))
-        for b in range(2, BLOCKS):
-            rows.append(load_block(b))
         res_sb = sb.tile([P, D], F32, name="res_sb")
         nc.sync.dma_start(res_sb[:], res)
-
         ident = sb.tile([P, P], F32, name="ident")
         make_identity(nc, ident[:])
-        size_ps = ps.tile([P, P], F32, name="size_ps", tag="gq_ps", bufs=2)
-        nc.tensor.transpose(size_ps[:], size_rows[:], ident[:])
-        size_cols = sb.tile([P, I // P], F32, name="size_cols")
-        nc.scalar.copy(size_cols[:], size_ps[:, 0 : I // P])
 
-        def quantise(name, grouped, width):
-            codes = sb.tile([P, width], U32, name=name + "_codes", align_bytes=64)
+        def quantise(name, grouped, width, tag):
+            codes = sb.tile([P, width], U32, name=name + "_codes", tag=tag, align_bytes=64)
             scales = sb.tile([P, width], U8, name=name + "_scales", align_bytes=64)
             nc.vector.quantize_mx(out=codes[:].bitcast(FP8X4), scales=scales[:], in_=grouped)
             return codes, scales
 
         def interleave(name, raw):
-            grouped = sb.tile([P, Q, PACK], BF16, name=name, align_bytes=64)
-            nc.scalar.copy(grouped[:], raw[:].rearrange("p j q -> p q j"))
+            grouped = sb.tile([P, Q, PACK], BF16, name=name, tag=name, align_bytes=64)
+            nc.scalar.activation(grouped[:], raw[:].rearrange("p j q -> p q j"), ACT.Copy)
             return grouped[:].rearrange("p q j -> p (q j)")
 
-        def gather(name, window, dtype):
-            picked = sb.tile([P, I], dtype, name=name, align_bytes=64)
+        def gather(name, window, dtype, tag):
+            picked = sb.tile([P, I], dtype, name=name, tag=tag, align_bytes=64)
             nc.vector.tensor_copy(picked[:], window[:].indirect(offsets[:]))
             return picked
 
         query_grouped = interleave("query_grouped", query_raw)
-        key_scales = gather("key_scales", key_plane, U8)
-        key_codes = gather("key_codes", key_words, U16)
-        q_codes, q_scales = quantise("q", query_grouped, Q)
-        a_ps = ps.tile([P, I], F32, name="a_ps")
+        key_scales = gather("key_scales", key_plane, U8, "key_scales")
+        key_codes = gather("key_codes", key_words, U16, "key_codes")
+        q_codes, q_scales = quantise("q", query_grouped, Q, "q_codes")
+        a_ps = ps.tile([P, I], F32, name="a_ps", tag="a_ps")
         nc.tensor.matmul_mx(out=a_ps[:], lhsT=q_codes[:].bitcast(FP8X4), lhsT_scale=q_scales[:],
                             rhs=key_codes[:].bitcast(FP4X4), rhs_scale=key_scales[:], start=True, stop=True)
 
         gout_grouped = interleave("gout_grouped", gout_raw)
-        val_codes = gather("val_codes", val_words, U16)
-        val_scales = gather("val_scales", val_plane, U8)
-        g_codes, g_scales = quantise("g", gout_grouped, Q)
-        c0t_ps = ps.tile([P, I // P, Q], F32, name="c0t_ps")
+        val_codes = gather("val_codes", val_words, U16, "query_grouped")
+        val_scales = gather("val_scales", val_plane, U8, "val_scales")
+        g_codes, g_scales = quantise("g", gout_grouped, Q, "g_codes")
+        c0t_ps = ps.tile([P, I // P, Q], F32, name="c0t_ps", tag="c0t_ps")
         for c in range(I // P):
             cols = slice(c * P, (c + 1) * P)
             nc.tensor.matmul_mx(out=c0t_ps[:, c, :], lhsT=val_codes[:, cols].bitcast(FP4X4), lhsT_scale=val_scales[:, cols],
                                 rhs=g_codes[:].bitcast(FP8X4), rhs_scale=g_scales[:], start=True, stop=True)
 
-        neg_slope = sb.tile([P, 1], F32, name="neg_slope")
-        nc.scalar.activation(neg_slope[:], steep_col[:], ACT.Copy, scale=-1.0 / PAGE)
-        slope = sb.tile([P, 1], F32, name="slope")
-        nc.scalar.activation(slope[:], steep_col[:], ACT.Copy, scale=1.0 / PAGE)
-        th_steep = sb.tile([P, 1], F32, name="th_steep")
-        nc.scalar.activation(th_steep[:], th_col[:], ACT.Copy, scale=steep_col[:])
+        gate_terms = sb.tile([P, 3], F32, name="gate_terms", tag="gout_raw")
+        neg_slope, slope, th_steep = gate_terms[:, 0:1], gate_terms[:, 1:2], gate_terms[:, 2:3]
+        nc.scalar.activation(neg_slope, steep_col[:], ACT.Copy, scale=-1.0 / PAGE)
+        nc.scalar.activation(th_steep, th_col[:], ACT.Copy, scale=steep_col[:])
+        nc.scalar.activation(slope, steep_col[:], ACT.Copy, scale=1.0 / PAGE)
 
-        page_sum = sb.tile([P, G], F32, name="page_sum")
-        nc.vector.tensor_reduce(page_sum[:], a_ps[:].rearrange("q (g j) -> q g j", j=PAGE), AXIS.X, ALU.add)
-        neg_max = sb.tile([P, 1], F32, name="neg_max")
-        nc.vector.tensor_reduce(neg_max[:], a_ps[:], AXIS.X, ALU.max, negate=True)
+        score_stats = sb.tile([P, G + 1], F32, name="score_stats", tag="val_plane", align_bytes=64)
+        page_sum, neg_max = score_stats[:, 0:G], score_stats[:, G : G + 1]
+        nc.vector.tensor_reduce(page_sum, a_ps[:].rearrange("q (g j) -> q g j", j=PAGE), AXIS.X, ALU.add)
+        nc.vector.tensor_reduce(neg_max, a_ps[:], AXIS.X, ALU.max, negate=True)
         odds = sb.tile([P, G], F32, name="odds")
-        nc.scalar.activation(odds[:], page_sum[:], ACT.Exp, bias=th_steep[:], scale=neg_slope[:])
-        denom = sb.tile([P, G], F32, name="denom")
+        nc.scalar.activation(odds[:], page_sum, ACT.Exp, bias=th_steep, scale=neg_slope)
+        denom = sb.tile([P, G], F32, name="denom", tag="denom", align_bytes=64)
         nc.scalar.activation(denom[:], odds[:], ACT.Identity, bias=1.0)
         r = sb.tile([P, PACK, P], F32, name="r")
-        nc.scalar.activation(r[:], a_ps[:].rearrange("q (s r) -> q r s", r=PACK), ACT.Exp, bias=neg_max[:])
+        nc.scalar.activation(r[:], a_ps[:].rearrange("q (s r) -> q r s", r=PACK), ACT.Exp, bias=neg_max)
         gate = sb.tile([P, G], F32, name="gate")
         nc.vector.reciprocal(gate[:], denom[:])
         gate4 = sb.tile([P, G, PACK], F32, name="gate4")
         nc.scalar.copy(gate4[:], gate[:].unsqueeze(2).broadcast_to([P, G, PACK]))
-        gate_slope = sb.tile([P, G], F32, name="gate_slope")
-        nc.scalar.activation(gate_slope[:], gate[:], ACT.Identity, bias=slope[:], scale=neg_slope[:])
 
-        ut = sb.tile([P, I // P, Q], F32, name="ut")
+        size_ps = ps.tile([P, P], F32, name="size_ps", tag="gq_ps", bufs=4)
+        nc.tensor.transpose(size_ps[:], size_rows[:], ident[:])
+        size_cols = sb.tile([P, I // P], F32, name="size_cols", tag="th_col")
+        nc.scalar.activation(size_cols[:], size_ps[:, 0 : I // P], ACT.Copy, scale=-1.0)
+        u_ps = ps.tile([P, I], F32, name="u_ps")
+        ut = sb.tile([P, I // P, Q], F32, name="ut", tag="val_plane", align_bytes=64)
         for c in range(I // P):
             nc.scalar.activation(ut[:, c, :], c0t_ps[:, c, :], ACT.Copy, scale=size_cols[:, c : c + 1])
-        u_ps = ps.tile([P, I], F32, name="u_ps")
         for c in range(I // P):
             nc.tensor.transpose(u_ps[:, c * P : (c + 1) * P], ut[:, c, :], ident[:])
 
-        p = sb.tile([P, PACK, P], F32, name="p")
-        z = sb.tile([P, 1], F32, name="z")
+        gate_slope = sb.tile([P, G], F32, name="gate_slope", tag="gate_slope", align_bytes=64)
+        nc.scalar.activation(gate_slope[:], gate[:], ACT.Identity, bias=slope, scale=neg_slope)
+
+        quantised_rows = []
+
+        def turn_rows(b):
+            picked = gather("picked%d" % b, rows[b], BF16, ("denom", "z", "pz", "gate_slope")[b])
+            pairs = picked[:].bitcast(F32)
+            kt_ps = ps.tile([P, 2, P], F32, name="kt_ps%d" % b, tag=("c0t_ps", "c0t_ps", "a_ps", "a_ps")[b])
+            for half in range(2):
+                nc.tensor.transpose(kt_ps[:, half, :], pairs[:, half : I // 2 : 2], ident[:])
+            kt_grouped = sb.tile([P, P * PACK], BF16, name="kt_grouped%d" % b, align_bytes=64)
+            nc.scalar.copy(kt_grouped[:].bitcast(F32).rearrange("s (d h) -> s d h", h=2), kt_ps[:].rearrange("s h d -> s d h"))
+            return kt_grouped
+
+        def quantise_rows(b, kt_grouped):
+            quantised_rows.append(quantise("kt%d" % b, kt_grouped[:], P, ("pu_sum", "rows1", "rows2", "kt3_codes")[b]))
+
+        turned = [turn_rows(0)]
+        p = sb.tile([P, PACK, P], F32, name="p", tag="rows0", align_bytes=64)
+        z = sb.tile([P, 1], F32, name="z", tag="z", align_bytes=64)
         gate_slots = gate4[:].rearrange("q g j -> q (g j)").unsqueeze(1).broadcast_to([P, PACK, P])
         nc.vector.scalar_tensor_tensor(p[:], r[:], 1.0, gate_slots, ALU.mult, ALU.mult, accum_out=z[:])
         inv_z = sb.tile([P, 1], F32, name="inv_z")
         nc.vector.reciprocal(inv_z[:], z[:])
+        pz = sb.tile([P, PACK, P], F32, name="pz", tag="pz", align_bytes=64)
+        nc.scalar.activation(pz[:], p[:], ACT.Copy, scale=inv_z[:])
         pu = sb.tile([P, PACK, P], F32, name="pu")
-        pu_sum = sb.tile([P, 1], F32, name="pu_sum")
+        pu_sum = sb.tile([P, 1], F32, name="pu_sum", tag="pu_sum", align_bytes=64)
         nc.vector.scalar_tensor_tensor(pu[:], u_ps[:].rearrange("q (s r) -> q r s", r=PACK), inv_z[:], p[:],
                                        ALU.mult, ALU.mult, accum_out=pu_sum[:])
-        dz = sb.tile([P, 1], F32, name="dz")
-        nc.vector.tensor_scalar(dz[:], pu_sum[:], inv_z[:], -1.0, ALU.mult, ALU.mult)
-        w = sb.tile([P, PACK, P], F32, name="w")
-        nc.vector.scalar_tensor_tensor(w[:], p[:], dz[:], pu[:], ALU.mult, ALU.add)
-        w_page = sb.tile([P, G], F32, name="w_page")
+        turned.append(turn_rows(1))
+        w = sb.tile([P, PACK, P], F32, name="w", tag="rows1", align_bytes=64)
+        nc.vector.scalar_tensor_tensor(w[:], pz[:], pu_sum[:], pu[:], ALU.mult, ALU.subtract)
+        turned.append(turn_rows(2))
+        w_page = sb.tile([P, G], F32, name="w_page", tag="rows2", align_bytes=64)
         nc.vector.tensor_reduce(w_page[:], w[:].rearrange("q r (g j) -> q g r j", j=PACK), AXIS.XY, ALU.add)
         r1 = sb.tile([P, G, PACK], F32, name="r1")
         nc.vector.tensor_tensor(r1[:], w_page[:].unsqueeze(2).broadcast_to([P, G, PACK]),
@@ -174,26 +191,19 @@ def tile_attend_bpagegate_q_kernel(tc, query, keys_words, keys_scales, th, steep
         for place in range(PACK):
             nc.tensor.matmul(dat_ps[:, place, :], r1[:].rearrange("q g j -> q (g j)"), ident[:],
                              start=False, stop=(place == PACK - 1), is_transpose=True)
-        gs_grouped = sb.tile([P, Q, PACK], BF16, name="gs_grouped", align_bytes=64)
+        turned.append(turn_rows(3))
+        gs_grouped = sb.tile([P, Q, PACK], BF16, name="gs_grouped", tag="rows3", align_bytes=64)
         nc.vector.tensor_tensor(gs_grouped[:], dat_ps[:].rearrange("s r q -> s q r"),
                                 fs_cols[:].unsqueeze(1).broadcast_to([P, Q, PACK]), ALU.mult)
-        gs_codes, gs_scales = quantise("gs", gs_grouped[:].rearrange("s q r -> s (q r)"), Q)
-
-        quantised_rows = []
+        gs_codes, gs_scales = quantise("gs", gs_grouped[:].rearrange("s q r -> s (q r)"), Q, "gs_codes")
         for b in range(BLOCKS):
-            picked = gather("picked%d" % b, rows[b], BF16)
-            pairs = picked[:].bitcast(F32)
-            kt_ps = ps.tile([P, 2, P], F32, name="kt_ps", tag="kt_ps", bufs=2)
-            for half in range(2):
-                nc.tensor.transpose(kt_ps[:, half, :], pairs[:, half : I // 2 : 2], ident[:])
-            kt_grouped = sb.tile([P, P * PACK], BF16, name="kt_grouped%d" % b, align_bytes=64)
-            nc.scalar.copy(kt_grouped[:].bitcast(F32).rearrange("s (d h) -> s d h", h=2), kt_ps[:].rearrange("s h d -> s d h"))
-            quantised_rows.append(quantise("kt%d" % b, kt_grouped[:], P))
+            quantise_rows(b, turned[b])
+
 
         for b in range(BLOCKS):
             cols = slice(b * P, (b + 1) * P)
             kt_codes, kt_scales = quantised_rows[b]
-            gq_ps = ps.tile([P, P], F32, name="gq_ps", tag="gq_ps", bufs=2)
+            gq_ps = ps.tile([P, P], F32, name="gq_ps", tag="gq_ps", bufs=4)
             nc.tensor.matmul_mx(out=gq_ps[:], lhsT=gs_codes[:].bitcast(FP8X4), lhsT_scale=gs_scales[:],
                                 rhs=kt_codes[:].bitcast(FP8X4), rhs_scale=kt_scales[:], start=True, stop=True)
             y = sb.tile([P, P], F32, name="y%d" % b)

@@ -45,7 +45,7 @@ def tile_attend_bpagegate_q_kernel(tc, query, keys_words, keys_scales, th, steep
             return pool_words
 
         def load_rows(name, rows):
-            raw = sb.tile([P, PACK, Q], F32, name=name, tag=name)
+            raw = sb.tile([P, PACK, Q], F32, name=name, tag=name, align_bytes=64)
             nc.sync.dma_start(raw[:], rows.rearrange("(p j) q -> p j q", j=PACK))
             return raw
 
@@ -104,54 +104,53 @@ def tile_attend_bpagegate_q_kernel(tc, query, keys_words, keys_scales, th, steep
                             rhs=key_codes[:].bitcast(FP4X4), rhs_scale=key_scales[:], start=True, stop=True)
 
         gout_grouped = interleave("gout_grouped", gout_raw)
-        val_codes = gather("val_codes", val_words, U16, "query_grouped")
-        val_scales = gather("val_scales", val_plane, U8, "val_scales")
-        g_codes, g_scales = quantise("g", gout_grouped, Q, "g_codes")
+        val_codes = gather("val_codes", val_words, U16, "query_raw")
+
+        gate_terms = sb.tile([P, 2], F32, name="gate_terms", tag="query_grouped", align_bytes=64)
+        neg_slope, th_steep = gate_terms[:, 0:1], gate_terms[:, 1:2]
+        nc.scalar.activation(neg_slope, steep_col[:], ACT.Copy, scale=-1.0 / PAGE)
+        nc.scalar.activation(th_steep, th_col[:], ACT.Copy, scale=steep_col[:])
+
+        page_sum = sb.tile([P, G], F32, name="page_sum", tag="page_sum", align_bytes=64)
+        neg_max = sb.tile([P, 1], F32, name="neg_max", tag="neg_max", align_bytes=64)
+        nc.vector.tensor_reduce(page_sum[:], a_ps[:].rearrange("q (g j) -> q g j", j=PAGE), AXIS.X, ALU.add)
+        nc.vector.tensor_reduce(neg_max[:], a_ps[:], AXIS.X, ALU.max, negate=True)
+        odds = sb.tile([P, G], F32, name="odds", tag="odds", align_bytes=64)
+        nc.scalar.activation(odds[:], page_sum[:], ACT.Exp, bias=th_steep, scale=neg_slope)
+        denom = sb.tile([P, G], F32, name="denom")
+        nc.scalar.activation(denom[:], odds[:], ACT.Identity, bias=1.0)
+        r = sb.tile([P, PACK, P], F32, name="r", tag="r", align_bytes=64)
+        nc.scalar.activation(r[:], a_ps[:].rearrange("q (s r) -> q r s", r=PACK), ACT.Exp, bias=neg_max[:])
+        val_scales = gather("val_scales", val_plane, U8, "page_sum")
+        gate = sb.tile([P, G], F32, name="gate")
+        nc.vector.reciprocal(gate[:], denom[:])
+        g_codes, g_scales = quantise("g", gout_grouped, Q, "odds")
         c0t_ps = ps.tile([P, I // P, Q], F32, name="c0t_ps", tag="c0t_ps")
         for c in range(I // P):
             cols = slice(c * P, (c + 1) * P)
             nc.tensor.matmul_mx(out=c0t_ps[:, c, :], lhsT=val_codes[:, cols].bitcast(FP4X4), lhsT_scale=val_scales[:, cols],
                                 rhs=g_codes[:].bitcast(FP8X4), rhs_scale=g_scales[:], start=True, stop=True)
-
-        gate_terms = sb.tile([P, 3], F32, name="gate_terms", tag="gout_raw")
-        neg_slope, slope, th_steep = gate_terms[:, 0:1], gate_terms[:, 1:2], gate_terms[:, 2:3]
-        nc.scalar.activation(neg_slope, steep_col[:], ACT.Copy, scale=-1.0 / PAGE)
-        nc.scalar.activation(th_steep, th_col[:], ACT.Copy, scale=steep_col[:])
-        nc.scalar.activation(slope, steep_col[:], ACT.Copy, scale=1.0 / PAGE)
-
-        score_stats = sb.tile([P, G + 1], F32, name="score_stats", tag="val_plane", align_bytes=64)
-        page_sum, neg_max = score_stats[:, 0:G], score_stats[:, G : G + 1]
-        nc.vector.tensor_reduce(page_sum, a_ps[:].rearrange("q (g j) -> q g j", j=PAGE), AXIS.X, ALU.add)
-        nc.vector.tensor_reduce(neg_max, a_ps[:], AXIS.X, ALU.max, negate=True)
-        odds = sb.tile([P, G], F32, name="odds")
-        nc.scalar.activation(odds[:], page_sum, ACT.Exp, bias=th_steep, scale=neg_slope)
-        denom = sb.tile([P, G], F32, name="denom", tag="denom", align_bytes=64)
-        nc.scalar.activation(denom[:], odds[:], ACT.Identity, bias=1.0)
-        r = sb.tile([P, PACK, P], F32, name="r")
-        nc.scalar.activation(r[:], a_ps[:].rearrange("q (s r) -> q r s", r=PACK), ACT.Exp, bias=neg_max)
-        gate = sb.tile([P, G], F32, name="gate")
-        nc.vector.reciprocal(gate[:], denom[:])
         gate4 = sb.tile([P, G, PACK], F32, name="gate4")
         nc.scalar.copy(gate4[:], gate[:].unsqueeze(2).broadcast_to([P, G, PACK]))
 
-        size_ps = ps.tile([P, P], F32, name="size_ps", tag="gq_ps", bufs=4)
+        size_ps = ps.tile([P, P], F32, name="size_ps")
         nc.tensor.transpose(size_ps[:], size_rows[:], ident[:])
         size_cols = sb.tile([P, I // P], F32, name="size_cols", tag="th_col")
         nc.scalar.activation(size_cols[:], size_ps[:, 0 : I // P], ACT.Copy, scale=-1.0)
         u_ps = ps.tile([P, I], F32, name="u_ps")
-        ut = sb.tile([P, I // P, Q], F32, name="ut", tag="val_plane", align_bytes=64)
+        ut = sb.tile([P, I // P, Q], F32, name="ut", tag="ut", align_bytes=64)
         for c in range(I // P):
             nc.scalar.activation(ut[:, c, :], c0t_ps[:, c, :], ACT.Copy, scale=size_cols[:, c : c + 1])
         for c in range(I // P):
             nc.tensor.transpose(u_ps[:, c * P : (c + 1) * P], ut[:, c, :], ident[:])
 
-        gate_slope = sb.tile([P, G], F32, name="gate_slope", tag="gate_slope", align_bytes=64)
-        nc.scalar.activation(gate_slope[:], gate[:], ACT.Identity, bias=slope, scale=neg_slope)
+        gate_less_one = sb.tile([P, G], F32, name="gate_less_one")
+        nc.scalar.activation(gate_less_one[:], gate[:], ACT.Identity, bias=-1.0)
 
         quantised_rows = []
 
         def turn_rows(b):
-            picked = gather("picked%d" % b, rows[b], BF16, ("denom", "z", "pz", "gate_slope")[b])
+            picked = gather("picked%d" % b, rows[b], BF16, ("neg_max", "r", "ut", "w")[b])
             pairs = picked[:].bitcast(F32)
             kt_ps = ps.tile([P, 2, P], F32, name="kt_ps%d" % b, tag=("c0t_ps", "c0t_ps", "a_ps", "a_ps")[b])
             for half in range(2):
@@ -161,30 +160,30 @@ def tile_attend_bpagegate_q_kernel(tc, query, keys_words, keys_scales, th, steep
             return kt_grouped
 
         def quantise_rows(b, kt_grouped):
-            quantised_rows.append(quantise("kt%d" % b, kt_grouped[:], P, ("pu_sum", "rows1", "rows2", "kt3_codes")[b]))
+            quantised_rows.append(quantise("kt%d" % b, kt_grouped[:], P, ("rows2", "pu_sum", "w_page", "kt3_codes")[b]))
 
         turned = [turn_rows(0)]
-        p = sb.tile([P, PACK, P], F32, name="p", tag="rows0", align_bytes=64)
-        z = sb.tile([P, 1], F32, name="z", tag="z", align_bytes=64)
+        p = sb.tile([P, PACK, P], F32, name="p")
+        z = sb.tile([P, 1], F32, name="z")
         gate_slots = gate4[:].rearrange("q g j -> q (g j)").unsqueeze(1).broadcast_to([P, PACK, P])
         nc.vector.scalar_tensor_tensor(p[:], r[:], 1.0, gate_slots, ALU.mult, ALU.mult, accum_out=z[:])
         inv_z = sb.tile([P, 1], F32, name="inv_z")
         nc.vector.reciprocal(inv_z[:], z[:])
-        pz = sb.tile([P, PACK, P], F32, name="pz", tag="pz", align_bytes=64)
+        turned.append(turn_rows(1))
+        pz = sb.tile([P, PACK, P], F32, name="pz")
         nc.scalar.activation(pz[:], p[:], ACT.Copy, scale=inv_z[:])
         pu = sb.tile([P, PACK, P], F32, name="pu")
         pu_sum = sb.tile([P, 1], F32, name="pu_sum", tag="pu_sum", align_bytes=64)
         nc.vector.scalar_tensor_tensor(pu[:], u_ps[:].rearrange("q (s r) -> q r s", r=PACK), inv_z[:], p[:],
                                        ALU.mult, ALU.mult, accum_out=pu_sum[:])
-        turned.append(turn_rows(1))
-        w = sb.tile([P, PACK, P], F32, name="w", tag="rows1", align_bytes=64)
-        nc.vector.scalar_tensor_tensor(w[:], pz[:], pu_sum[:], pu[:], ALU.mult, ALU.subtract)
         turned.append(turn_rows(2))
-        w_page = sb.tile([P, G], F32, name="w_page", tag="rows2", align_bytes=64)
+        w = sb.tile([P, PACK, P], F32, name="w", tag="w", align_bytes=64)
+        nc.vector.scalar_tensor_tensor(w[:], pz[:], pu_sum[:], pu[:], ALU.mult, ALU.subtract)
+        w_page = sb.tile([P, G], F32, name="w_page", tag="w_page", align_bytes=64)
         nc.vector.tensor_reduce(w_page[:], w[:].rearrange("q r (g j) -> q g r j", j=PACK), AXIS.XY, ALU.add)
         r1 = sb.tile([P, G, PACK], F32, name="r1")
-        nc.vector.tensor_tensor(r1[:], w_page[:].unsqueeze(2).broadcast_to([P, G, PACK]),
-                                gate_slope[:].unsqueeze(2).broadcast_to([P, G, PACK]), ALU.mult)
+        nc.vector.scalar_tensor_tensor(r1[:], gate_less_one[:].unsqueeze(2).broadcast_to([P, G, PACK]), neg_slope,
+                                       w_page[:].unsqueeze(2).broadcast_to([P, G, PACK]), ALU.mult, ALU.mult)
         dat_ps = ps.tile([P, PACK, Q], F32, name="dat_ps")
         for place in range(PACK):
             nc.tensor.matmul(dat_ps[:, place, :], w[:, place, :], ident[:], start=(place == 0), stop=False, is_transpose=True)
@@ -192,7 +191,7 @@ def tile_attend_bpagegate_q_kernel(tc, query, keys_words, keys_scales, th, steep
             nc.tensor.matmul(dat_ps[:, place, :], r1[:].rearrange("q g j -> q (g j)"), ident[:],
                              start=False, stop=(place == PACK - 1), is_transpose=True)
         turned.append(turn_rows(3))
-        gs_grouped = sb.tile([P, Q, PACK], BF16, name="gs_grouped", tag="rows3", align_bytes=64)
+        gs_grouped = sb.tile([P, Q, PACK], BF16, name="gs_grouped", align_bytes=64)
         nc.vector.tensor_tensor(gs_grouped[:], dat_ps[:].rearrange("s r q -> s q r"),
                                 fs_cols[:].unsqueeze(1).broadcast_to([P, Q, PACK]), ALU.mult)
         gs_codes, gs_scales = quantise("gs", gs_grouped[:].rearrange("s q r -> s (q r)"), Q, "gs_codes")
@@ -200,12 +199,14 @@ def tile_attend_bpagegate_q_kernel(tc, query, keys_words, keys_scales, th, steep
             quantise_rows(b, turned[b])
 
 
-        for b in range(BLOCKS):
-            cols = slice(b * P, (b + 1) * P)
-            kt_codes, kt_scales = quantised_rows[b]
-            gq_ps = ps.tile([P, P], F32, name="gq_ps", tag="gq_ps", bufs=4)
-            nc.tensor.matmul_mx(out=gq_ps[:], lhsT=gs_codes[:].bitcast(FP8X4), lhsT_scale=gs_scales[:],
-                                rhs=kt_codes[:].bitcast(FP8X4), rhs_scale=kt_scales[:], start=True, stop=True)
-            y = sb.tile([P, P], F32, name="y%d" % b)
+        for first, last in ((0, BLOCKS - 1), (BLOCKS - 1, BLOCKS)):
+            cols = slice(first * P, last * P)
+            gq_ps = ps.tile([P, (last - first) * P], F32, name="gq_ps%d" % first)
+            for b in range(first, last):
+                kt_codes, kt_scales = quantised_rows[b]
+                nc.tensor.matmul_mx(out=gq_ps[:, (b - first) * P : (b - first + 1) * P],
+                                    lhsT=gs_codes[:].bitcast(FP8X4), lhsT_scale=gs_scales[:],
+                                    rhs=kt_codes[:].bitcast(FP8X4), rhs_scale=kt_scales[:], start=True, stop=True)
+            y = sb.tile([P, (last - first) * P], F32, name="y%d" % first)
             nc.vector.tensor_tensor(y[:], gq_ps[:], res_sb[:, cols], ALU.add)
             nc.sync.dma_start(out[:, cols], y[:])

@@ -22,6 +22,7 @@ P = 128
 PACK = 4
 PAGE = I // G
 BLOCKS = D // P
+SCALAR_BLOCK = 2
 
 
 def tile_attend_bpagegate_q_kernel(tc, query, keys_words, keys_scales, th, steep, gout, vals_words, vals_scales,
@@ -65,14 +66,14 @@ def tile_attend_bpagegate_q_kernel(tc, query, keys_words, keys_scales, th, steep
         nc.sync.dma_start(size_rows[0 : I // P, :], size.rearrange("o (c p) -> (o c) p", p=P))
         val_plane = load_scales("val_plane", vals_scales, nc.vector)
         gout_raw = load_rows("gout_raw", gout)
-        rows = [load_block(0)]
+        rows = {SCALAR_BLOCK: load_block(SCALAR_BLOCK)}
         steep_col = sb.tile([P, 1], F32, name="steep_col")
         nc.gpsimd.dma_start(steep_col[:], steep)
-        th_col = sb.tile([P, 1], F32, name="th_col", tag="th_col")
+        th_col = sb.tile([P, 1], F32, name="th_col", tag="th_col", align_bytes=64)
         nc.gpsimd.dma_start(th_col[:], th)
-        for b in range(1, BLOCKS):
-            rows.append(load_block(b))
-        fs_cols = sb.tile([P, PACK], F32, name="fs_cols")
+        for b in (0, 1, 3):
+            rows[b] = load_block(b)
+        fs_cols = sb.tile([P, PACK], F32, name="fs_cols", tag="fs_cols", align_bytes=64)
         nc.sync.dma_start(fs_cols[:], fs.rearrange("o (p r) -> p (o r)", r=PACK))
         res_sb = sb.tile([P, D], F32, name="res_sb")
         nc.sync.dma_start(res_sb[:], res)
@@ -112,7 +113,7 @@ def tile_attend_bpagegate_q_kernel(tc, query, keys_words, keys_scales, th, steep
         nc.scalar.activation(th_steep, th_col[:], ACT.Copy, scale=steep_col[:])
 
         page_sum = sb.tile([P, G], F32, name="page_sum", tag="page_sum", align_bytes=64)
-        neg_max = sb.tile([P, 1], F32, name="neg_max", tag="neg_max", align_bytes=64)
+        neg_max = sb.tile([P, 1], F32, name="neg_max")
         nc.vector.tensor_reduce(page_sum[:], a_ps[:].rearrange("q (g j) -> q g j", j=PAGE), AXIS.X, ALU.add)
         nc.vector.tensor_reduce(neg_max[:], a_ps[:], AXIS.X, ALU.max, negate=True)
         odds = sb.tile([P, G], F32, name="odds", tag="odds", align_bytes=64)
@@ -122,7 +123,7 @@ def tile_attend_bpagegate_q_kernel(tc, query, keys_words, keys_scales, th, steep
         r = sb.tile([P, PACK, P], F32, name="r", tag="r", align_bytes=64)
         nc.scalar.activation(r[:], a_ps[:].rearrange("q (s r) -> q r s", r=PACK), ACT.Exp, bias=neg_max[:])
         val_scales = gather("val_scales", val_plane, U8, "page_sum")
-        gate = sb.tile([P, G], F32, name="gate")
+        gate = sb.tile([P, G], F32, name="gate", tag="gate", align_bytes=64)
         nc.vector.reciprocal(gate[:], denom[:])
         g_codes, g_scales = quantise("g", gout_grouped, Q, "odds")
         c0t_ps = ps.tile([P, I // P, Q], F32, name="c0t_ps", tag="c0t_ps")
@@ -133,50 +134,49 @@ def tile_attend_bpagegate_q_kernel(tc, query, keys_words, keys_scales, th, steep
         gate4 = sb.tile([P, G, PACK], F32, name="gate4")
         nc.scalar.copy(gate4[:], gate[:].unsqueeze(2).broadcast_to([P, G, PACK]))
 
-        size_ps = ps.tile([P, P], F32, name="size_ps")
+        size_ps = ps.tile([P, P], F32, name="size_ps", tag="size_ps")
         nc.tensor.transpose(size_ps[:], size_rows[:], ident[:])
-        size_cols = sb.tile([P, I // P], F32, name="size_cols", tag="th_col")
+        size_cols = sb.tile([P, I // P], F32, name="size_cols", tag="th_col", align_bytes=64)
         nc.scalar.activation(size_cols[:], size_ps[:, 0 : I // P], ACT.Copy, scale=-1.0)
-        u_ps = ps.tile([P, I], F32, name="u_ps")
-        ut = sb.tile([P, I // P, Q], F32, name="ut", tag="ut", align_bytes=64)
-        for c in range(I // P):
-            nc.scalar.activation(ut[:, c, :], c0t_ps[:, c, :], ACT.Copy, scale=size_cols[:, c : c + 1])
-        for c in range(I // P):
-            nc.tensor.transpose(u_ps[:, c * P : (c + 1) * P], ut[:, c, :], ident[:])
 
         gate_less_one = sb.tile([P, G], F32, name="gate_less_one")
         nc.scalar.activation(gate_less_one[:], gate[:], ACT.Identity, bias=-1.0)
 
-        quantised_rows = []
-
-        def turn_rows(b):
-            picked = gather("picked%d" % b, rows[b], BF16, ("neg_max", "r", "ut", "w")[b])
+        def turn_rows(b, picked, bank):
             pairs = picked[:].bitcast(F32)
-            kt_ps = ps.tile([P, 2, P], F32, name="kt_ps%d" % b, tag=("c0t_ps", "c0t_ps", "a_ps", "a_ps")[b])
+            kt_ps = ps.tile([P, 2, P], F32, name="kt_ps%d" % b, tag=bank)
             for half in range(2):
                 nc.tensor.transpose(kt_ps[:, half, :], pairs[:, half : I // 2 : 2], ident[:])
             kt_grouped = sb.tile([P, P * PACK], BF16, name="kt_grouped%d" % b, align_bytes=64)
             nc.scalar.copy(kt_grouped[:].bitcast(F32).rearrange("s (d h) -> s d h", h=2), kt_ps[:].rearrange("s h d -> s d h"))
             return kt_grouped
 
-        def quantise_rows(b, kt_grouped):
-            quantised_rows.append(quantise("kt%d" % b, kt_grouped[:], P, ("rows2", "pu_sum", "w_page", "kt3_codes")[b]))
-
-        turned = [turn_rows(0)]
+        turned = {}
         p = sb.tile([P, PACK, P], F32, name="p")
-        z = sb.tile([P, 1], F32, name="z")
+        z = sb.tile([P, 1], F32, name="z", tag="z", align_bytes=64)
         gate_slots = gate4[:].rearrange("q g j -> q (g j)").unsqueeze(1).broadcast_to([P, PACK, P])
         nc.vector.scalar_tensor_tensor(p[:], r[:], 1.0, gate_slots, ALU.mult, ALU.mult, accum_out=z[:])
         inv_z = sb.tile([P, 1], F32, name="inv_z")
         nc.vector.reciprocal(inv_z[:], z[:])
-        turned.append(turn_rows(1))
         pz = sb.tile([P, PACK, P], F32, name="pz")
         nc.scalar.activation(pz[:], p[:], ACT.Copy, scale=inv_z[:])
-        pu = sb.tile([P, PACK, P], F32, name="pu")
-        pu_sum = sb.tile([P, 1], F32, name="pu_sum", tag="pu_sum", align_bytes=64)
+        u_ps = ps.tile([P, I], F32, name="u_ps", tag="u_ps")
+        ut = sb.tile([P, I // P, Q], F32, name="ut", tag="z", align_bytes=64)
+        for c in range(I // P):
+            nc.scalar.activation(ut[:, c, :], c0t_ps[:, c, :], ACT.Copy, scale=size_cols[:, c : c + 1])
+        for c in range(I // P):
+            nc.tensor.transpose(u_ps[:, c * P : (c + 1) * P], ut[:, c, :], ident[:])
+        turned[0] = turn_rows(0, gather("picked0", rows[0], BF16, "r"), "c0t_ps")
+        turned[1] = turn_rows(1, gather("picked1", rows[1], BF16, "picked1"), "a_ps")
+        rows_bf16 = sb.tile([P, T], BF16, name="rows_bf16", tag="gate", align_bytes=64)
+        for cols in (slice(0, T // 2), slice(T // 2, T)):
+            nc.scalar.activation(rows_bf16[:, cols], rows[SCALAR_BLOCK][:, cols], ACT.Copy)
+        picked2 = sb.tile([P, I], BF16, name="picked2", align_bytes=64)
+        nc.scalar.activation(picked2[:], rows_bf16[:].indirect(offsets[:]), ACT.Copy)
+        pu = sb.tile([P, PACK, P], F32, name="pu", tag="rows1", align_bytes=64)
+        pu_sum = sb.tile([P, 1], F32, name="pu_sum")
         nc.vector.scalar_tensor_tensor(pu[:], u_ps[:].rearrange("q (s r) -> q r s", r=PACK), inv_z[:], p[:],
                                        ALU.mult, ALU.mult, accum_out=pu_sum[:])
-        turned.append(turn_rows(2))
         w = sb.tile([P, PACK, P], F32, name="w", tag="w", align_bytes=64)
         nc.vector.scalar_tensor_tensor(w[:], pz[:], pu_sum[:], pu[:], ALU.mult, ALU.subtract)
         w_page = sb.tile([P, G], F32, name="w_page", tag="w_page", align_bytes=64)
@@ -190,16 +190,17 @@ def tile_attend_bpagegate_q_kernel(tc, query, keys_words, keys_scales, th, steep
         for place in range(PACK):
             nc.tensor.matmul(dat_ps[:, place, :], r1[:].rearrange("q g j -> q (g j)"), ident[:],
                              start=False, stop=(place == PACK - 1), is_transpose=True)
-        turned.append(turn_rows(3))
+        turned[2] = turn_rows(2, picked2, "u_ps")
+        turned[3] = turn_rows(3, gather("picked3", rows[3], BF16, "w"), "size_ps")
         gs_grouped = sb.tile([P, Q, PACK], BF16, name="gs_grouped", align_bytes=64)
         nc.vector.tensor_tensor(gs_grouped[:], dat_ps[:].rearrange("s r q -> s q r"),
                                 fs_cols[:].unsqueeze(1).broadcast_to([P, Q, PACK]), ALU.mult)
         gs_codes, gs_scales = quantise("gs", gs_grouped[:].rearrange("s q r -> s (q r)"), Q, "gs_codes")
-        for b in range(BLOCKS):
-            quantise_rows(b, turned[b])
+        quantised_rows = [quantise("kt%d" % b, turned[b][:], P, tag)
+                          for b, tag in enumerate(("w_page", "rows3", "fs_cols", "kt3_codes"))]
 
 
-        for first, last in ((0, BLOCKS - 1), (BLOCKS - 1, BLOCKS)):
+        for first, last in ((0, 2), (2, 4)):
             cols = slice(first * P, last * P)
             gq_ps = ps.tile([P, (last - first) * P], F32, name="gq_ps%d" % first)
             for b in range(first, last):

from contextlib import ExitStack

import concourse.mybir as mybir
from concourse.masks import make_identity

D, E, T, I, Q, G = 512, 512, 2048, 512, 128, 32
FLOPS = 2 * Q * I * (D + E + D)

F32 = mybir.dt.float32
BF16 = mybir.dt.bfloat16
I32 = mybir.dt.int32
U32 = mybir.dt.uint32
U16 = mybir.dt.uint16
U8 = mybir.dt.uint8
FP8X4 = mybir.dt.float8_e4m3fn_x4
FP4X4 = mybir.dt.float4_e2m1fn_x4
ALU = mybir.AluOpType
ACT = mybir.ActivationFunctionType
AXIS = mybir.AxisListType

P = 128
PACK = 4
PAGE = I // G
BLOCKS = D // P
SCALAR_BLOCK = 2


def tile_attend_bpagegate_q_kernel(tc, query, keys_words, keys_scales, th, steep, gout, vals_words, vals_scales,
                                    size, fs, keyrows, res, offs, out):
    nc = tc.nc
    with ExitStack() as ctx:
        sb = ctx.enter_context(tc.tile_pool(name="sb", bufs=1))
        ps = ctx.enter_context(tc.psum_pool(name="ps", bufs=1))

        def load_scales(name, scales, engine):
            plane = sb.tile([P, T], U8, name=name, tag=name, align_bytes=64)
            engine.memset(plane[:].bitcast(I32), 0)
            for quad in range(4):
                nc.sync.dma_start(plane[32 * quad : 32 * quad + 4, :].bitcast(I32),
                                  scales[0, 4 * quad : 4 * quad + 4, :].bitcast(I32))
            return plane

        def load_words(name, words):
            pool_words = sb.tile([P, T], U16, name=name, align_bytes=64)
            nc.sync.dma_start(pool_words[:].bitcast(I32), words[0].bitcast(I32))
            return pool_words

        def load_rows(name, rows):
            raw = sb.tile([P, PACK, Q], F32, name=name, tag=name, align_bytes=64)
            nc.sync.dma_start(raw[:], rows.rearrange("(p j) q -> p j q", j=PACK))
            return raw

        def load_block(b):
            block = sb.tile([P, T], F32, name="rows%d" % b, tag="rows%d" % b, align_bytes=64)
            nc.sync.dma_start(block[:], keyrows[b * P : (b + 1) * P, :])
            return block

        offsets = sb.tile([P, I // 16], U16, name="offsets")
        nc.sync.dma_start(offsets[:], offs)
        key_plane = load_scales("key_plane", keys_scales, nc.gpsimd)
        key_words = load_words("key_words", keys_words)
        query_raw = load_rows("query_raw", query)
        val_words = load_words("val_words", vals_words)
        size_rows = sb.tile([P, P], F32, name="size_rows")
        nc.vector.memset(size_rows[:], 0.0)
        nc.sync.dma_start(size_rows[0 : I // P, :], size.rearrange("o (c p) -> (o c) p", p=P))
        val_plane = load_scales("val_plane", vals_scales, nc.vector)
        gout_raw = load_rows("gout_raw", gout)
        rows = {SCALAR_BLOCK: load_block(SCALAR_BLOCK)}
        steep_col = sb.tile([P, 1], F32, name="steep_col")
        nc.gpsimd.dma_start(steep_col[:], steep)
        th_col = sb.tile([P, 1], F32, name="th_col", tag="th_col", align_bytes=64)
        nc.gpsimd.dma_start(th_col[:], th)
        for b in (0, 1, 3):
            rows[b] = load_block(b)
        fs_cols = sb.tile([P, PACK], F32, name="fs_cols", tag="fs_cols", align_bytes=64)
        nc.sync.dma_start(fs_cols[:], fs.rearrange("o (p r) -> p (o r)", r=PACK))
        res_sb = sb.tile([P, D], F32, name="res_sb")
        nc.sync.dma_start(res_sb[:], res)
        ident = sb.tile([P, P], F32, name="ident")
        make_identity(nc, ident[:])

        def quantise(name, grouped, width, tag):
            codes = sb.tile([P, width], U32, name=name + "_codes", tag=tag, align_bytes=64)
            scales = sb.tile([P, width], U8, name=name + "_scales", align_bytes=64)
            nc.vector.quantize_mx(out=codes[:].bitcast(FP8X4), scales=scales[:], in_=grouped)
            return codes, scales

        def interleave(name, raw):
            grouped = sb.tile([P, Q, PACK], BF16, name=name, tag=name, align_bytes=64)
            nc.scalar.activation(grouped[:], raw[:].rearrange("p j q -> p q j"), ACT.Copy)
            return grouped[:].rearrange("p q j -> p (q j)")

        def gather(name, window, dtype, tag):
            picked = sb.tile([P, I], dtype, name=name, tag=tag, align_bytes=64)
            nc.vector.tensor_copy(picked[:], window[:].indirect(offsets[:]))
            return picked

        query_grouped = interleave("query_grouped", query_raw)
        key_scales = gather("key_scales", key_plane, U8, "key_scales")
        key_codes = gather("key_codes", key_words, U16, "key_codes")
        q_codes, q_scales = quantise("q", query_grouped, Q, "q_codes")
        a_ps = ps.tile([P, I], F32, name="a_ps", tag="a_ps")
        nc.tensor.matmul_mx(out=a_ps[:], lhsT=q_codes[:].bitcast(FP8X4), lhsT_scale=q_scales[:],
                            rhs=key_codes[:].bitcast(FP4X4), rhs_scale=key_scales[:], start=True, stop=True)

        gout_grouped = interleave("gout_grouped", gout_raw)
        val_codes = gather("val_codes", val_words, U16, "query_raw")

        gate_terms = sb.tile([P, 2], F32, name="gate_terms", tag="query_grouped", align_bytes=64)
        neg_slope, th_steep = gate_terms[:, 0:1], gate_terms[:, 1:2]
        nc.scalar.activation(neg_slope, steep_col[:], ACT.Copy, scale=-1.0 / PAGE)
        nc.scalar.activation(th_steep, th_col[:], ACT.Copy, scale=steep_col[:])

        page_sum = sb.tile([P, G], F32, name="page_sum", tag="page_sum", align_bytes=64)
        neg_max = sb.tile([P, 1], F32, name="neg_max")
        nc.vector.tensor_reduce(page_sum[:], a_ps[:].rearrange("q (g j) -> q g j", j=PAGE), AXIS.X, ALU.add)
        nc.vector.tensor_reduce(neg_max[:], a_ps[:], AXIS.X, ALU.max, negate=True)
        odds = sb.tile([P, G], F32, name="odds", tag="odds", align_bytes=64)
        nc.scalar.activation(odds[:], page_sum[:], ACT.Exp, bias=th_steep, scale=neg_slope)
        denom = sb.tile([P, G], F32, name="denom")
        nc.scalar.activation(denom[:], odds[:], ACT.Identity, bias=1.0)
        r = sb.tile([P, PACK, P], F32, name="r", tag="r", align_bytes=64)
        nc.scalar.activation(r[:], a_ps[:].rearrange("q (s r) -> q r s", r=PACK), ACT.Exp, bias=neg_max[:])
        val_scales = gather("val_scales", val_plane, U8, "page_sum")
        gate = sb.tile([P, G], F32, name="gate", tag="gate", align_bytes=64)
        nc.vector.reciprocal(gate[:], denom[:])
        g_codes, g_scales = quantise("g", gout_grouped, Q, "odds")
        c0t_ps = ps.tile([P, I // P, Q], F32, name="c0t_ps", tag="c0t_ps")
        for c in range(I // P):
            cols = slice(c * P, (c + 1) * P)
            nc.tensor.matmul_mx(out=c0t_ps[:, c, :], lhsT=val_codes[:, cols].bitcast(FP4X4), lhsT_scale=val_scales[:, cols],
                                rhs=g_codes[:].bitcast(FP8X4), rhs_scale=g_scales[:], start=True, stop=True)
        gate4 = sb.tile([P, G, PACK], F32, name="gate4")
        nc.scalar.copy(gate4[:], gate[:].unsqueeze(2).broadcast_to([P, G, PACK]))

        size_ps = ps.tile([P, P], F32, name="size_ps", tag="size_ps")
        nc.tensor.transpose(size_ps[:], size_rows[:], ident[:])
        size_cols = sb.tile([P, I // P], F32, name="size_cols", tag="th_col", align_bytes=64)
        nc.scalar.activation(size_cols[:], size_ps[:, 0 : I // P], ACT.Copy, scale=-1.0)

        gate_less_one = sb.tile([P, G], F32, name="gate_less_one")
        nc.scalar.activation(gate_less_one[:], gate[:], ACT.Identity, bias=-1.0)

        def turn_rows(b, picked, bank):
            pairs = picked[:].bitcast(F32)
            kt_ps = ps.tile([P, 2, P], F32, name="kt_ps%d" % b, tag=bank)
            for half in range(2):
                nc.tensor.transpose(kt_ps[:, half, :], pairs[:, half : I // 2 : 2], ident[:])
            kt_grouped = sb.tile([P, P * PACK], BF16, name="kt_grouped%d" % b, align_bytes=64)
            nc.scalar.copy(kt_grouped[:].bitcast(F32).rearrange("s (d h) -> s d h", h=2), kt_ps[:].rearrange("s h d -> s d h"))
            return kt_grouped

        turned = {}
        p = sb.tile([P, PACK, P], F32, name="p")
        z = sb.tile([P, 1], F32, name="z", tag="z", align_bytes=64)
        gate_slots = gate4[:].rearrange("q g j -> q (g j)").unsqueeze(1).broadcast_to([P, PACK, P])
        nc.vector.scalar_tensor_tensor(p[:], r[:], 1.0, gate_slots, ALU.mult, ALU.mult, accum_out=z[:])
        inv_z = sb.tile([P, 1], F32, name="inv_z")
        nc.vector.reciprocal(inv_z[:], z[:])
        pz = sb.tile([P, PACK, P], F32, name="pz")
        nc.scalar.activation(pz[:], p[:], ACT.Copy, scale=inv_z[:])
        u_ps = ps.tile([P, I], F32, name="u_ps", tag="u_ps")
        ut = sb.tile([P, I // P, Q], F32, name="ut", tag="z", align_bytes=64)
        for c in range(I // P):
            nc.scalar.activation(ut[:, c, :], c0t_ps[:, c, :], ACT.Copy, scale=size_cols[:, c : c + 1])
        for c in range(I // P):
            nc.tensor.transpose(u_ps[:, c * P : (c + 1) * P], ut[:, c, :], ident[:])
        turned[0] = turn_rows(0, gather("picked0", rows[0], BF16, "r"), "c0t_ps")
        turned[1] = turn_rows(1, gather("picked1", rows[1], BF16, "picked1"), "a_ps")
        rows_bf16 = sb.tile([P, T], BF16, name="rows_bf16", tag="gate", align_bytes=64)
        for cols in (slice(0, T // 2), slice(T // 2, T)):
            nc.scalar.activation(rows_bf16[:, cols], rows[SCALAR_BLOCK][:, cols], ACT.Copy)
        picked2 = sb.tile([P, I], BF16, name="picked2", align_bytes=64)
        nc.scalar.activation(picked2[:], rows_bf16[:].indirect(offsets[:]), ACT.Copy)
        pu = sb.tile([P, PACK, P], F32, name="pu", tag="rows1", align_bytes=64)
        pu_sum = sb.tile([P, 1], F32, name="pu_sum")
        nc.vector.scalar_tensor_tensor(pu[:], u_ps[:].rearrange("q (s r) -> q r s", r=PACK), inv_z[:], p[:],
                                       ALU.mult, ALU.mult, accum_out=pu_sum[:])
        w = sb.tile([P, PACK, P], F32, name="w", tag="w", align_bytes=64)
        nc.vector.scalar_tensor_tensor(w[:], pz[:], pu_sum[:], pu[:], ALU.mult, ALU.subtract)
        w_page = sb.tile([P, G], F32, name="w_page", tag="w_page", align_bytes=64)
        nc.vector.tensor_reduce(w_page[:], w[:].rearrange("q r (g j) -> q g r j", j=PACK), AXIS.XY, ALU.add)
        r1 = sb.tile([P, G, PACK], F32, name="r1")
        nc.vector.scalar_tensor_tensor(r1[:], gate_less_one[:].unsqueeze(2).broadcast_to([P, G, PACK]), neg_slope,
                                       w_page[:].unsqueeze(2).broadcast_to([P, G, PACK]), ALU.mult, ALU.mult)
        dat_ps = ps.tile([P, PACK, Q], F32, name="dat_ps")
        for place in range(PACK):
            nc.tensor.matmul(dat_ps[:, place, :], w[:, place, :], ident[:], start=(place == 0), stop=False, is_transpose=True)
        for place in range(PACK):
            nc.tensor.matmul(dat_ps[:, place, :], r1[:].rearrange("q g j -> q (g j)"), ident[:],
                             start=False, stop=(place == PACK - 1), is_transpose=True)
        turned[2] = turn_rows(2, picked2, "u_ps")
        turned[3] = turn_rows(3, gather("picked3", rows[3], BF16, "w"), "size_ps")
        gs_grouped = sb.tile([P, Q, PACK], BF16, name="gs_grouped", align_bytes=64)
        nc.vector.tensor_tensor(gs_grouped[:], dat_ps[:].rearrange("s r q -> s q r"),
                                fs_cols[:].unsqueeze(1).broadcast_to([P, Q, PACK]), ALU.mult)
        gs_codes, gs_scales = quantise("gs", gs_grouped[:].rearrange("s q r -> s (q r)"), Q, "gs_codes")
        quantised_rows = [quantise("kt%d" % b, turned[b][:], P, tag)
                          for b, tag in enumerate(("w_page", "rows3", "fs_cols", "kt3_codes"))]


        for first, last in ((0, 2), (2, 4)):
            cols = slice(first * P, last * P)
            gq_ps = ps.tile([P, (last - first) * P], F32, name="gq_ps%d" % first)
            for b in range(first, last):
                kt_codes, kt_scales = quantised_rows[b]
                nc.tensor.matmul_mx(out=gq_ps[:, (b - first) * P : (b - first + 1) * P],
                                    lhsT=gs_codes[:].bitcast(FP8X4), lhsT_scale=gs_scales[:],
                                    rhs=kt_codes[:].bitcast(FP8X4), rhs_scale=kt_scales[:], start=True, stop=True)
            y = sb.tile([P, (last - first) * P], F32, name="y%d" % first)
            nc.vector.tensor_tensor(y[:], gq_ps[:], res_sb[:, cols], ALU.add)
            nc.sync.dma_start(out[:, cols], y[:])
